import numpy as np
import ml_dtypes


def mxq(x, axis, fmt="e4m3"):
    dtype, down = {"e4m3": (ml_dtypes.float8_e4m3fn, 7), "e5m2": (ml_dtypes.float8_e5m2, 14)}[fmt]
    v = np.moveaxis(np.asarray(x, np.float32).astype(ml_dtypes.bfloat16).astype(np.float64), axis, -1)
    blocks = v.reshape(v.shape[:-1] + (-1, 32))
    amax = np.abs(blocks).max(-1, keepdims=True)
    byte = np.maximum(np.where(amax > 0, np.frexp(amax)[1] - 1 + 127, 0) - down, 1)
    scale = np.exp2(byte - 127.0)
    codes = (blocks / scale).astype(np.float32).astype(dtype).astype(np.float64)
    return np.moveaxis((codes * scale).reshape(v.shape), -1, axis)


WIDE = False


def mx_kscale(k):
    if not WIDE:
        return np.ones(k)
    levels = np.array([10, -10, 5, -5, 0])
    if k % 512:
        return np.exp2(np.random.permutation(np.resize(levels, k // 32))).repeat(32)
    a = np.empty((k // 512, 16))
    for p in range(k // 512):
        a[p, :8] = np.random.permutation(np.resize(levels, 8))
        for g in range(8):
            far = levels[np.abs(levels - a[p, g]) >= 10]
            a[p, g + 8] = far[np.random.randint(len(far))]
    return np.exp2(a.ravel()).repeat(32)


def f64(x):
    return np.asarray(x).astype(np.float64)


def striped(idx):
    return np.tile(idx.reshape(-1, 16).T, (8, 1)).astype(np.uint16)


def unstriped(offs):
    return offs[:16].T.reshape(-1).astype(np.int64)


def striped8(idx):
    return np.concatenate([x.reshape(-1, 16).T for x in idx]).astype(np.uint16)


def runs(offs, k):
    lists = np.stack([offs[16 * r : 16 * r + 16].T.reshape(-1) for r in range(8)]).astype(np.int64)
    return lists[np.arange(k) % 512 // 64]


def pack_weight(w):
    k, n = w.shape
    w = f64(np.asarray(w, np.float32).astype(ml_dtypes.bfloat16)).reshape(k // 32, 32, n)
    amax = np.abs(w).max(1)
    byte = np.clip(np.where(amax > 0, np.frexp(amax)[1] - 1 + 127 - 7, 1), 1, 254)
    scaled = (w * np.exp2(127.0 - byte)[:, None, :]).reshape(k, n).astype(np.float32)
    words = np.ascontiguousarray(scaled.reshape(k // 512, 128, 4, n).transpose(0, 1, 3, 2)).astype(ml_dtypes.float8_e4m3fn).view(np.uint8)
    return words, np.ascontiguousarray(byte.astype(np.uint8).reshape(k // 512, 16, n))


def unpack_weight(words, scales):
    g, p, n, _ = words.shape
    vals = np.ascontiguousarray(words).view(ml_dtypes.float8_e4m3fn).astype(np.float64) * np.repeat(np.exp2(scales.astype(np.float64) - 127.0), 8, axis=1)[..., None]
    return vals.transpose(0, 1, 3, 2).reshape(g * 512, n)


K, T, S, N, G, H = 512, 2048, 512, 512, 2048, 512


def setup_inputs():
    n = np.random.standard_normal
    s = mx_kscale(K)[:, None]
    u = mx_kscale(H)
    packed_xT = pack_weight(n((K, T)) * s)
    packed_dT = pack_weight(n((K, G)) / s)
    return {
        "x_words": packed_xT[0],
        "x_scales": packed_xT[1],
        "d_words": packed_dT[0],
        "d_scales": packed_dT[1],
        "gn": (np.random.uniform(0.5, 1.5, (H, 1)) * u[:, None]).astype(np.float32),
        "w1": (n((H, N)) / np.sqrt(H) / u[:, None]).astype(np.float32),
        "offs": striped(np.random.permutation(T)[:S]),
        "k1": striped8(np.random.randint(0, G, (8, H))),
        "k2": striped8(np.random.randint(0, G, (8, H))),
        "nb": striped8(np.stack([np.random.permutation(S) for _ in range(8)])),
    }


def reference(x_words, x_scales, d_words, d_scales, gn, w1, offs, k1, k2, nb):
    d_k1 = unpack_weight(d_words, d_scales)[np.arange(K)[:, None], runs(k1, K)]
    xq = unpack_weight(x_words, x_scales)[:, unstriped(offs)]
    a = 0.0625 * (d_k1.T @ xq)
    d_k2 = unpack_weight(d_words, d_scales)[np.arange(K)[:, None], runs(k2, K)]
    b = 0.0625 * (d_k2.T @ xq)
    z = f64(gn) * (a / (np.abs(b[np.arange(H)[:, None], runs(nb, H)]) + 0.5))
    return mxq(f64(w1), 0, "e4m3").T @ mxq(z, 0, "e4m3")

@@ -1,0 +1,209 @@
+from contextlib import ExitStack
+
+import concourse.mybir as mybir
+
+K, T, S, N, G, H = 512, 2048, 512, 512, 2048, 512
+FLOPS = 2 * K * H * S * 2 + 2 * H * N * S
+
+F32 = mybir.dt.float32
+BF16 = mybir.dt.bfloat16
+I32 = mybir.dt.int32
+U32 = mybir.dt.uint32
+U16 = mybir.dt.uint16
+U8 = mybir.dt.uint8
+FP8X4 = mybir.dt.float8_e4m3fn_x4
+ACT = mybir.ActivationFunctionType
+MULT = mybir.AluOpType.mult
+
+P = 128
+PACK = 4
+HALF = S // 2
+CHUNKS = [(0, 256), (256, 384), (384, 512)]
+VECTOR_TILES = (1, 2, 3)
+
+
+def tile_picked_scoredev2_none_p_kernel(
+    tc, x_words, x_scales, d_words, d_scales, gn, w1, offs, k1, k2, nb, out
+):
+    nc = tc.nc
+    with ExitStack() as ctx:
+        keep = ctx.enter_context(tc.tile_pool(name="keep", bufs=1))
+        psum = ctx.enter_context(tc.psum_pool(name="psum", bufs=1))
+
+        def new(shape, dtype, name, tag=""):
+            return keep.tile(shape, dtype, name=name, tag=tag, align_bytes=64)
+
+        def words_of(packed):
+            return packed[0].rearrange("p n t -> p (n t)").bitcast(I32)
+
+        offs_sb = new([P, S // 16], U16, "offs_sb")
+        k1_sb = new([P, H // 16], U16, "k1_sb")
+        k2_sb = new([P, H // 16], U16, "k2_sb")
+        nb_sb = new([P, S // 16], U16, "nb_sb")
+        d_table = new([P, G], U32, "d_table")
+        x_table = new([P, T], U32, "x_table")
+        d_bytes = new([P, G], U8, "d_bytes")
+        x_bytes = new([P, T], U8, "x_bytes")
+        gn_sb = new([P, PACK], F32, "gn_sb")
+
+        warm = new([P, 2], F32, "warm")
+        nc.vector.memset(warm[:, 0:1], 1.0)
+        nc.scalar.activation(warm[:, 1:2], warm[:, 0:1], ACT.Ln)
+
+        def x_scale_rows(q, queue):
+            queue.dma_start(
+                x_bytes[32 * q : 32 * q + 32, :].bitcast(I32),
+                x_scales[0][4 * q : 4 * q + 4, :].bitcast(I32).unsqueeze(0).broadcast_to([8, 4, T // 4]),
+            )
+
+        w_raw = new([P, PACK, N], F32, "w_raw")
+        nc.sync.dma_start(k2_sb[:], k2)
+        nc.scalar.dma_start(
+            d_bytes[:].bitcast(I32), d_scales[0].bitcast(I32).unsqueeze(1).broadcast_to([16, 8, G // 4])
+        )
+        nc.sync.dma_start(offs_sb[:], offs)
+        for q in range(3):
+            x_scale_rows(q, nc.scalar)
+        x_scale_rows(3, nc.sync)
+        nc.sync.dma_start(d_table[:].bitcast(I32), words_of(d_words))
+        nc.sync.dma_start(x_table[:].bitcast(I32), words_of(x_words))
+        nc.sync.dma_start(k1_sb[:], k1)
+        nc.sync.dma_start(nb_sb[:], nb)
+        nc.sync.dma_start(w_raw[:], w1.rearrange("(p t) n -> p t n", t=PACK))
+        nc.gpsimd.dma_start(gn_sb[:], gn.rearrange("(p t) o -> p (t o)", t=PACK))
+
+        def deal(dst, src, run):
+            nc.vector.tensor_copy(
+                dst[:].rearrange("p (t c i) -> p c t i", t=PACK, i=run),
+                src[:].rearrange("p (c i t) -> p c t i", t=PACK, i=run),
+            )
+
+        def key_scales(name, codes, queue):
+            picked = new([P, H], U8, name + "_bytes_picked")
+            dealt = new([P, H], U8, name + "_bytes_dealt")
+            plane = new([P, H], U8, name + "_plane")
+            nc.vector.tensor_copy(picked[:], d_bytes[:].indirect(codes[:]))
+            deal(dealt, picked, 16)
+            nc.vector.tensor_copy(plane[:].bitcast(I32), dealt[:].bitcast(I32))
+            for j in range(1, 4):
+                queue.dma_start(plane[j:P:32, :].bitcast(I32), dealt[8 * j : P : 32, :].bitcast(I32))
+            return plane
+
+        def key_words(name, codes):
+            picked = new([P, H], U32, name + "_words_picked")
+            dealt = new([P, H], U32, name + "_words_dealt")
+            nc.vector.tensor_copy(picked[:], d_table[:].indirect(codes[:]))
+            deal(dealt, picked, 4)
+            return dealt
+
+        def interleave(copy, dst, src):
+            copy(
+                dst.rearrange("p (c i t) -> p c t i", t=PACK, i=4),
+                src.rearrange("p t (c i) -> p c t i", i=4),
+            )
+
+        b_plane = key_scales("b", k2_sb, nc.scalar)
+        b_words = key_words("b", k2_sb)
+        xq_words = new([P, S], U32, "xq_words")
+        xq_plane = new([P, S], U8, "xq_plane")
+        mag = new([P, PACK, S], F32, "mag", tag="stage")
+        b_acc = [psum.tile([P, S], F32, name="b_acc%d" % t, tag="bank%d" % t) for t in range(PACK)]
+        for h in range(2):
+            cols = slice(h * HALF, (h + 1) * HALF)
+            part = offs_sb[:, cols.start // 16 : cols.stop // 16]
+            nc.vector.tensor_copy(xq_plane[:, cols], x_bytes[:].indirect(part))
+            nc.vector.tensor_copy(xq_words[:, cols], x_table[:].indirect(part))
+            for t in range(PACK):
+                keys = slice(t * P, (t + 1) * P)
+                nc.tensor.matmul_mx(
+                    out=b_acc[t][:, cols],
+                    lhsT=b_words[:, keys].bitcast(FP8X4),
+                    lhsT_scale=b_plane[:, keys],
+                    rhs=xq_words[:, cols].bitcast(FP8X4),
+                    rhs_scale=xq_plane[:, cols],
+                    start=True,
+                    stop=True,
+                )
+                nc.scalar.activation(mag[:, t, cols], b_acc[t][:, cols], ACT.Abs)
+
+        w_codes = new([P, N], U32, "w_codes")
+        w_plane = new([P, N], U8, "w_plane")
+        w_bf = new([P, PACK * N], BF16, "w_bf")
+
+        logs = [new([P, S], F32, "log%d" % t, tag="log%d" % t) for t in range(PACK)]
+        for t in range(PACK):
+            nc.scalar.activation(logs[t][:], mag[:, t, :], ACT.Ln, bias=8.0)
+
+        a_plane = key_scales("a", k1_sb, nc.sync)
+        a_words = key_words("a", k1_sb)
+        a_acc = [psum.tile([P, S], F32, name="a_acc%d" % t, tag="bank%d" % (PACK + t)) for t in range(PACK)]
+        for t in range(PACK):
+            keys = slice(t * P, (t + 1) * P)
+            nc.tensor.matmul_mx(
+                out=a_acc[t][:],
+                lhsT=a_words[:, keys].bitcast(FP8X4),
+                lhsT_scale=a_plane[:, keys],
+                rhs=xq_words[:].bitcast(FP8X4),
+                rhs_scale=xq_plane[:],
+                start=True,
+                stop=True,
+            )
+
+        interleave(nc.vector.tensor_copy, w_bf[:], w_raw[:])
+
+        first = slice(CHUNKS[0][0], CHUNKS[0][1])
+        logs_picked = new([P, len(VECTOR_TILES), first.stop - first.start], F32, "logs_picked", tag="later")
+        for v, t in enumerate(VECTOR_TILES):
+            nc.vector.tensor_copy(
+                logs_picked[:, v, :], logs[t][:].indirect(nb_sb[:, first.start // 16 : first.stop // 16])
+            )
+
+        nc.vector.quantize_mx(out=w_codes[:].bitcast(FP8X4), scales=w_plane[:], in_=w_bf[:])
+
+        recips = [new([P, PACK, HALF], F32, "recip%d" % h, tag=tag) for h, tag in enumerate(("stage", "later"))]
+        sums = []
+        out_rows = out.rearrange("(u p) j -> p u j", p=P)
+        for n, (lo, hi) in enumerate(CHUNKS):
+            cols = slice(lo, hi)
+            width = hi - lo
+            recip = recips[lo // HALF][:, :, lo % HALF : lo % HALF + width]
+            z_planes = new([P, PACK, width], BF16, "z_planes%d" % n, tag="z_planes")
+            z_bf = new([P, PACK * width], BF16, "z_bf%d" % n)
+            z_codes = new([P, width], U32, "z_codes%d" % n)
+            z_plane = new([P, width], U8, "z_plane%d" % n)
+            for t in range(PACK):
+                if n == 0 and t in VECTOR_TILES:
+                    source = logs_picked[:, VECTOR_TILES.index(t), :]
+                else:
+                    source = logs[t][:].indirect(nb_sb[:, lo // 16 : hi // 16])
+                nc.scalar.activation(recip[:, t, :], source, ACT.Exp, scale=-1.0)
+                nc.vector.scalar_tensor_tensor(
+                    z_planes[:, t, :], a_acc[t][:, cols], gn_sb[:, t : t + 1], recip[:, t, :], MULT, MULT
+                )
+            interleave(nc.vector.tensor_copy, z_bf[:], z_planes[:])
+            nc.vector.quantize_mx(out=z_codes[:].bitcast(FP8X4), scales=z_plane[:], in_=z_bf[:])
+            for pair in range(2):
+                acc = psum.tile([P, 2, width], F32, name="acc%d_%d" % (n, pair), tag="bank%d" % (2 * n + pair))
+                for v in range(2):
+                    rows = slice((2 * pair + v) * P, (2 * pair + v + 1) * P)
+                    nc.tensor.matmul_mx(
+                        out=acc[:, v, :],
+                        lhsT=w_codes[:, rows].bitcast(FP8X4),
+                        lhsT_scale=w_plane[:, rows],
+                        rhs=z_codes[:].bitcast(FP8X4),
+                        rhs_scale=z_plane[:],
+                        start=True,
+                        stop=True,
+                    )
+                sums.append(acc)
+
+        for n, (lo, hi) in enumerate(CHUNKS[:-1]):
+            staged = new([P, PACK, hi - lo], F32, "staged%d" % n, tag="log%d" % (PACK - 1 - n))
+            for pair in range(2):
+                nc.scalar.copy(staged[:, 2 * pair : 2 * pair + 2, :], sums[2 * n + pair][:])
+            nc.sync.dma_start(out_rows[:, :, lo:hi], staged[:])
+        lo, hi = CHUNKS[-1]
+        for pair, (copy, queue) in enumerate(((nc.vector.tensor_copy, nc.sync), (nc.scalar.copy, nc.scalar))):
+            staged = new([P, 2, hi - lo], F32, "staged_last%d" % pair)
+            copy(staged[:], sums[2 * len(CHUNKS) - 2 + pair][:])
+            queue.dma_start(out_rows[:, 2 * pair : 2 * pair + 2, lo:hi], staged[:])

@@ -41,36 +41,26 @@ def tile_picked_scoredev2_none_p_kernel(
         k2_sb = new([P, H // 16], U16, "k2_sb")
         nb_sb = new([P, S // 16], U16, "nb_sb")
         d_table = new([P, G], U32, "d_table")
-        x_table = new([P, T], U32, "x_table")
+        x_table = new([P, T], U32, "x_table", tag="x_table")
         d_bytes = new([P, G], U8, "d_bytes")
         x_bytes = new([P, T], U8, "x_bytes")
         gn_sb = new([P, PACK], F32, "gn_sb")
 
-        warm = new([P, 2], F32, "warm")
-        nc.vector.memset(warm[:, 0:1], 1.0)
-        nc.scalar.activation(warm[:, 1:2], warm[:, 0:1], ACT.Ln)
-
-        def x_scale_rows(q, queue):
-            queue.dma_start(
-                x_bytes[32 * q : 32 * q + 32, :].bitcast(I32),
-                x_scales[0][4 * q : 4 * q + 4, :].bitcast(I32).unsqueeze(0).broadcast_to([8, 4, T // 4]),
-            )
-
-        w_raw = new([P, PACK, N], F32, "w_raw")
-        nc.sync.dma_start(k2_sb[:], k2)
+        nc.vector.memset(x_bytes[:].bitcast(I32), 0)
+        for tile, source in ((k2_sb, k2), (offs_sb, offs), (k1_sb, k1), (nb_sb, nb)):
+            nc.sync.dma_start(tile[:], source)
         nc.scalar.dma_start(
             d_bytes[:].bitcast(I32), d_scales[0].bitcast(I32).unsqueeze(1).broadcast_to([16, 8, G // 4])
         )
-        nc.sync.dma_start(offs_sb[:], offs)
-        for q in range(3):
-            x_scale_rows(q, nc.scalar)
-        x_scale_rows(3, nc.sync)
         nc.sync.dma_start(d_table[:].bitcast(I32), words_of(d_words))
+        for j in range(4):
+            nc.scalar.dma_start(x_bytes[j:P:32, :].bitcast(I32), x_scales[0][j:16:4, :].bitcast(I32))
         nc.sync.dma_start(x_table[:].bitcast(I32), words_of(x_words))
-        nc.sync.dma_start(k1_sb[:], k1)
-        nc.sync.dma_start(nb_sb[:], nb)
-        nc.sync.dma_start(w_raw[:], w1.rearrange("(p t) n -> p t n", t=PACK))
         nc.gpsimd.dma_start(gn_sb[:], gn.rearrange("(p t) o -> p (t o)", t=PACK))
+
+        warm = new([P, 2], F32, "warm")
+        nc.vector.memset(warm[:, 0:1], 1.0)
+        nc.scalar.activation(warm[:, 1:2], warm[:, 0:1], ACT.Ln)
 
         def deal(dst, src, run):
             nc.vector.tensor_copy(
@@ -78,19 +68,17 @@ def tile_picked_scoredev2_none_p_kernel(
                 src[:].rearrange("p (c i t) -> p c t i", t=PACK, i=run),
             )
 
-        def key_scales(name, codes, queue):
-            picked = new([P, H], U8, name + "_bytes_picked")
-            dealt = new([P, H], U8, name + "_bytes_dealt")
+        def key_scales(name, codes, queue, picked_tag):
+            picked = new([P, H], U8, name + "_bytes_picked", tag=picked_tag)
             plane = new([P, H], U8, name + "_plane")
             nc.vector.tensor_copy(picked[:], d_bytes[:].indirect(codes[:]))
-            deal(dealt, picked, 16)
-            nc.vector.tensor_copy(plane[:].bitcast(I32), dealt[:].bitcast(I32))
+            deal(plane, picked, 16)
             for j in range(1, 4):
-                queue.dma_start(plane[j:P:32, :].bitcast(I32), dealt[8 * j : P : 32, :].bitcast(I32))
+                queue.dma_start(plane[j:P:32, :].bitcast(I32), plane[8 * j : P : 32, :].bitcast(I32))
             return plane
 
-        def key_words(name, codes):
-            picked = new([P, H], U32, name + "_words_picked")
+        def key_words(name, codes, picked_tag):
+            picked = new([P, H], U32, name + "_words_picked", tag=picked_tag)
             dealt = new([P, H], U32, name + "_words_dealt")
             nc.vector.tensor_copy(picked[:], d_table[:].indirect(codes[:]))
             deal(dealt, picked, 4)
@@ -102,29 +90,32 @@ def tile_picked_scoredev2_none_p_kernel(
                 src.rearrange("p t (c i) -> p c t i", i=4),
             )
 
-        b_plane = key_scales("b", k2_sb, nc.scalar)
-        b_words = key_words("b", k2_sb)
+        b_plane = key_scales("b", k2_sb, nc.scalar, "")
+        b_words = key_words("b", k2_sb, "w_raw")
+        w_raw = new([P, PACK, N], F32, "w_raw", tag="w_raw")
+        nc.sync.dma_start(w_raw[:], w1.rearrange("(p t) n -> p t n", t=PACK))
         xq_words = new([P, S], U32, "xq_words")
         xq_plane = new([P, S], U8, "xq_plane")
         mag = new([P, PACK, S], F32, "mag", tag="stage")
-        b_acc = [psum.tile([P, S], F32, name="b_acc%d" % t, tag="bank%d" % t) for t in range(PACK)]
         for h in range(2):
             cols = slice(h * HALF, (h + 1) * HALF)
             part = offs_sb[:, cols.start // 16 : cols.stop // 16]
             nc.vector.tensor_copy(xq_plane[:, cols], x_bytes[:].indirect(part))
             nc.vector.tensor_copy(xq_words[:, cols], x_table[:].indirect(part))
-            for t in range(PACK):
-                keys = slice(t * P, (t + 1) * P)
-                nc.tensor.matmul_mx(
-                    out=b_acc[t][:, cols],
-                    lhsT=b_words[:, keys].bitcast(FP8X4),
-                    lhsT_scale=b_plane[:, keys],
-                    rhs=xq_words[:, cols].bitcast(FP8X4),
-                    rhs_scale=xq_plane[:, cols],
-                    start=True,
-                    stop=True,
-                )
-                nc.scalar.activation(mag[:, t, cols], b_acc[t][:, cols], ACT.Abs)
+            for pair in range(2):
+                b_acc = psum.tile([P, 2, HALF], F32, name="b_acc%d_%d" % (h, pair), tag="bank%d" % (2 * h + pair))
+                for v in range(2):
+                    keys = slice((2 * pair + v) * P, (2 * pair + v + 1) * P)
+                    nc.tensor.matmul_mx(
+                        out=b_acc[:, v, :],
+                        lhsT=b_words[:, keys].bitcast(FP8X4),
+                        lhsT_scale=b_plane[:, keys],
+                        rhs=xq_words[:, cols].bitcast(FP8X4),
+                        rhs_scale=xq_plane[:, cols],
+                        start=True,
+                        stop=True,
+                    )
+                nc.scalar.activation(mag[:, 2 * pair : 2 * pair + 2, cols], b_acc[:], ACT.Abs)
 
         w_codes = new([P, N], U32, "w_codes")
         w_plane = new([P, N], U8, "w_plane")
@@ -134,8 +125,8 @@ def tile_picked_scoredev2_none_p_kernel(
         for t in range(PACK):
             nc.scalar.activation(logs[t][:], mag[:, t, :], ACT.Ln, bias=8.0)
 
-        a_plane = key_scales("a", k1_sb, nc.sync)
-        a_words = key_words("a", k1_sb)
+        a_plane = key_scales("a", k1_sb, nc.sync, "x_table")
+        a_words = key_words("a", k1_sb, "x_table")
         a_acc = [psum.tile([P, S], F32, name="a_acc%d" % t, tag="bank%d" % (PACK + t)) for t in range(PACK)]
         for t in range(PACK):
             keys = slice(t * P, (t + 1) * P)
@@ -157,7 +148,6 @@ def tile_picked_scoredev2_none_p_kernel(
             nc.vector.tensor_copy(
                 logs_picked[:, v, :], logs[t][:].indirect(nb_sb[:, first.start // 16 : first.stop // 16])
             )
-
         nc.vector.quantize_mx(out=w_codes[:].bitcast(FP8X4), scales=w_plane[:], in_=w_bf[:])
 
         recips = [new([P, PACK, HALF], F32, "recip%d" % h, tag=tag) for h, tag in enumerate(("stage", "later"))]

@@ -44,7 +44,6 @@ def tile_picked_scoredev2_none_p_kernel(
         x_table = new([P, T], U32, "x_table", tag="x_table")
         d_bytes = new([P, G], U8, "d_bytes")
         x_bytes = new([P, T], U8, "x_bytes")
-        gn_sb = new([P, PACK], F32, "gn_sb")
 
         nc.vector.memset(x_bytes[:].bitcast(I32), 0)
         for tile, source in ((k2_sb, k2), (offs_sb, offs), (k1_sb, k1), (nb_sb, nb)):
@@ -56,7 +55,6 @@ def tile_picked_scoredev2_none_p_kernel(
         for j in range(4):
             nc.scalar.dma_start(x_bytes[j:P:32, :].bitcast(I32), x_scales[0][j:16:4, :].bitcast(I32))
         nc.sync.dma_start(x_table[:].bitcast(I32), words_of(x_words))
-        nc.gpsimd.dma_start(gn_sb[:], gn.rearrange("(p t) o -> p (t o)", t=PACK))
 
         warm = new([P, 2], F32, "warm")
         nc.vector.memset(warm[:, 0:1], 1.0)
@@ -90,7 +88,9 @@ def tile_picked_scoredev2_none_p_kernel(
                 src.rearrange("p t (c i) -> p c t i", i=4),
             )
 
-        b_plane = key_scales("b", k2_sb, nc.scalar, "")
+        b_plane = key_scales("b", k2_sb, nc.scalar, "gn")
+        gn_sb = new([P, PACK], F32, "gn_sb", tag="gn")
+        nc.scalar.dma_start(gn_sb[:], gn.rearrange("(p t) o -> p (t o)", t=PACK))
         b_words = key_words("b", k2_sb, "w_raw")
         w_raw = new([P, PACK, N], F32, "w_raw", tag="w_raw")
         nc.sync.dma_start(w_raw[:], w1.rearrange("(p t) n -> p t n", t=PACK))

from contextlib import ExitStack

import concourse.mybir as mybir

K, T, S, N, G, H = 512, 2048, 512, 512, 2048, 512
FLOPS = 2 * K * H * S * 2 + 2 * H * N * S

F32 = mybir.dt.float32
BF16 = mybir.dt.bfloat16
I32 = mybir.dt.int32
U32 = mybir.dt.uint32
U16 = mybir.dt.uint16
U8 = mybir.dt.uint8
FP8X4 = mybir.dt.float8_e4m3fn_x4
ACT = mybir.ActivationFunctionType
MULT = mybir.AluOpType.mult

P = 128
PACK = 4
HALF = S // 2
CHUNKS = [(0, 256), (256, 384), (384, 512)]
VECTOR_TILES = (1, 2, 3)


def tile_picked_scoredev2_none_p_kernel(
    tc, x_words, x_scales, d_words, d_scales, gn, w1, offs, k1, k2, nb, out
):
    nc = tc.nc
    with ExitStack() as ctx:
        keep = ctx.enter_context(tc.tile_pool(name="keep", bufs=1))
        psum = ctx.enter_context(tc.psum_pool(name="psum", bufs=1))

        def new(shape, dtype, name, tag=""):
            return keep.tile(shape, dtype, name=name, tag=tag, align_bytes=64)

        def words_of(packed):
            return packed[0].rearrange("p n t -> p (n t)").bitcast(I32)

        offs_sb = new([P, S // 16], U16, "offs_sb")
        k1_sb = new([P, H // 16], U16, "k1_sb")
        k2_sb = new([P, H // 16], U16, "k2_sb")
        nb_sb = new([P, S // 16], U16, "nb_sb")
        d_table = new([P, G], U32, "d_table")
        x_table = new([P, T], U32, "x_table", tag="x_table")
        d_bytes = new([P, G], U8, "d_bytes")
        x_bytes = new([P, T], U8, "x_bytes")

        nc.vector.memset(x_bytes[:].bitcast(I32), 0)
        for tile, source in ((k2_sb, k2), (offs_sb, offs), (k1_sb, k1), (nb_sb, nb)):
            nc.sync.dma_start(tile[:], source)
        nc.scalar.dma_start(
            d_bytes[:].bitcast(I32), d_scales[0].bitcast(I32).unsqueeze(1).broadcast_to([16, 8, G // 4])
        )
        nc.sync.dma_start(d_table[:].bitcast(I32), words_of(d_words))
        for j in range(4):
            nc.scalar.dma_start(x_bytes[j:P:32, :].bitcast(I32), x_scales[0][j:16:4, :].bitcast(I32))
        nc.sync.dma_start(x_table[:].bitcast(I32), words_of(x_words))

        warm = new([P, 2], F32, "warm")
        nc.vector.memset(warm[:, 0:1], 1.0)
        nc.scalar.activation(warm[:, 1:2], warm[:, 0:1], ACT.Ln)

        def deal(dst, src, run):
            nc.vector.tensor_copy(
                dst[:].rearrange("p (t c i) -> p c t i", t=PACK, i=run),
                src[:].rearrange("p (c i t) -> p c t i", t=PACK, i=run),
            )

        def key_scales(name, codes, queue, picked_tag):
            picked = new([P, H], U8, name + "_bytes_picked", tag=picked_tag)
            plane = new([P, H], U8, name + "_plane")
            nc.vector.tensor_copy(picked[:], d_bytes[:].indirect(codes[:]))
            deal(plane, picked, 16)
            for j in range(1, 4):
                queue.dma_start(plane[j:P:32, :].bitcast(I32), plane[8 * j : P : 32, :].bitcast(I32))
            return plane

        def key_words(name, codes, picked_tag):
            picked = new([P, H], U32, name + "_words_picked", tag=picked_tag)
            dealt = new([P, H], U32, name + "_words_dealt")
            nc.vector.tensor_copy(picked[:], d_table[:].indirect(codes[:]))
            deal(dealt, picked, 4)
            return dealt

        def interleave(copy, dst, src):
            copy(
                dst.rearrange("p (c i t) -> p c t i", t=PACK, i=4),
                src.rearrange("p t (c i) -> p c t i", i=4),
            )

        b_plane = key_scales("b", k2_sb, nc.scalar, "gn")
        gn_sb = new([P, PACK], F32, "gn_sb", tag="gn")
        nc.scalar.dma_start(gn_sb[:], gn.rearrange("(p t) o -> p (t o)", t=PACK))
        b_words = key_words("b", k2_sb, "w_raw")
        w_raw = new([P, PACK, N], F32, "w_raw", tag="w_raw")
        nc.sync.dma_start(w_raw[:], w1.rearrange("(p t) n -> p t n", t=PACK))
        xq_words = new([P, S], U32, "xq_words")
        xq_plane = new([P, S], U8, "xq_plane")
        mag = new([P, PACK, S], F32, "mag", tag="stage")
        for h in range(2):
            cols = slice(h * HALF, (h + 1) * HALF)
            part = offs_sb[:, cols.start // 16 : cols.stop // 16]
            nc.vector.tensor_copy(xq_plane[:, cols], x_bytes[:].indirect(part))
            nc.vector.tensor_copy(xq_words[:, cols], x_table[:].indirect(part))
            for pair in range(2):
                b_acc = psum.tile([P, 2, HALF], F32, name="b_acc%d_%d" % (h, pair), tag="bank%d" % (2 * h + pair))
                for v in range(2):
                    keys = slice((2 * pair + v) * P, (2 * pair + v + 1) * P)
                    nc.tensor.matmul_mx(
                        out=b_acc[:, v, :],
                        lhsT=b_words[:, keys].bitcast(FP8X4),
                        lhsT_scale=b_plane[:, keys],
                        rhs=xq_words[:, cols].bitcast(FP8X4),
                        rhs_scale=xq_plane[:, cols],
                        start=True,
                        stop=True,
                    )
                nc.scalar.activation(mag[:, 2 * pair : 2 * pair + 2, cols], b_acc[:], ACT.Abs)

        w_codes = new([P, N], U32, "w_codes")
        w_plane = new([P, N], U8, "w_plane")
        w_bf = new([P, PACK * N], BF16, "w_bf")

        logs = [new([P, S], F32, "log%d" % t, tag="log%d" % t) for t in range(PACK)]
        for t in range(PACK):
            nc.scalar.activation(logs[t][:], mag[:, t, :], ACT.Ln, bias=8.0)

        a_plane = key_scales("a", k1_sb, nc.sync, "x_table")
        a_words = key_words("a", k1_sb, "x_table")
        a_acc = [psum.tile([P, S], F32, name="a_acc%d" % t, tag="bank%d" % (PACK + t)) for t in range(PACK)]
        for t in range(PACK):
            keys = slice(t * P, (t + 1) * P)
            nc.tensor.matmul_mx(
                out=a_acc[t][:],
                lhsT=a_words[:, keys].bitcast(FP8X4),
                lhsT_scale=a_plane[:, keys],
                rhs=xq_words[:].bitcast(FP8X4),
                rhs_scale=xq_plane[:],
                start=True,
                stop=True,
            )

        interleave(nc.vector.tensor_copy, w_bf[:], w_raw[:])

        first = slice(CHUNKS[0][0], CHUNKS[0][1])
        logs_picked = new([P, len(VECTOR_TILES), first.stop - first.start], F32, "logs_picked", tag="later")
        for v, t in enumerate(VECTOR_TILES):
            nc.vector.tensor_copy(
                logs_picked[:, v, :], logs[t][:].indirect(nb_sb[:, first.start // 16 : first.stop // 16])
            )
        nc.vector.quantize_mx(out=w_codes[:].bitcast(FP8X4), scales=w_plane[:], in_=w_bf[:])

        recips = [new([P, PACK, HALF], F32, "recip%d" % h, tag=tag) for h, tag in enumerate(("stage", "later"))]
        sums = []
        out_rows = out.rearrange("(u p) j -> p u j", p=P)
        for n, (lo, hi) in enumerate(CHUNKS):
            cols = slice(lo, hi)
            width = hi - lo
            recip = recips[lo // HALF][:, :, lo % HALF : lo % HALF + width]
            z_planes = new([P, PACK, width], BF16, "z_planes%d" % n, tag="z_planes")
            z_bf = new([P, PACK * width], BF16, "z_bf%d" % n)
            z_codes = new([P, width], U32, "z_codes%d" % n)
            z_plane = new([P, width], U8, "z_plane%d" % n)
            for t in range(PACK):
                if n == 0 and t in VECTOR_TILES:
                    source = logs_picked[:, VECTOR_TILES.index(t), :]
                else:
                    source = logs[t][:].indirect(nb_sb[:, lo // 16 : hi // 16])
                nc.scalar.activation(recip[:, t, :], source, ACT.Exp, scale=-1.0)
                nc.vector.scalar_tensor_tensor(
                    z_planes[:, t, :], a_acc[t][:, cols], gn_sb[:, t : t + 1], recip[:, t, :], MULT, MULT
                )
            interleave(nc.vector.tensor_copy, z_bf[:], z_planes[:])
            nc.vector.quantize_mx(out=z_codes[:].bitcast(FP8X4), scales=z_plane[:], in_=z_bf[:])
            for pair in range(2):
                acc = psum.tile([P, 2, width], F32, name="acc%d_%d" % (n, pair), tag="bank%d" % (2 * n + pair))
                for v in range(2):
                    rows = slice((2 * pair + v) * P, (2 * pair + v + 1) * P)
                    nc.tensor.matmul_mx(
                        out=acc[:, v, :],
                        lhsT=w_codes[:, rows].bitcast(FP8X4),
                        lhsT_scale=w_plane[:, rows],
                        rhs=z_codes[:].bitcast(FP8X4),
                        rhs_scale=z_plane[:],
                        start=True,
                        stop=True,
                    )
                sums.append(acc)

        for n, (lo, hi) in enumerate(CHUNKS[:-1]):
            staged = new([P, PACK, hi - lo], F32, "staged%d" % n, tag="log%d" % (PACK - 1 - n))
            for pair in range(2):
                nc.scalar.copy(staged[:, 2 * pair : 2 * pair + 2, :], sums[2 * n + pair][:])
            nc.sync.dma_start(out_rows[:, :, lo:hi], staged[:])
        lo, hi = CHUNKS[-1]
        for pair, (copy, queue) in enumerate(((nc.vector.tensor_copy, nc.sync), (nc.scalar.copy, nc.scalar))):
            staged = new([P, 2, hi - lo], F32, "staged_last%d" % pair)
            copy(staged[:], sums[2 * len(CHUNKS) - 2 + pair][:])
            queue.dma_start(out_rows[:, 2 * pair : 2 * pair + 2, lo:hi], staged[:])
